import numpy as np
import ml_dtypes

BF16 = ml_dtypes.bfloat16


def bf(x):
    return np.asarray(x, np.float32).astype(BF16)


def f32(x):
    return np.asarray(x, np.float32)


def f64(x):
    return np.asarray(x).astype(np.float64)


def striped(idx):
    return np.tile(idx.reshape(-1, 16).T, (8, 1))


S, K, M, N, D, V = 2048, 256, 128, 1024, 4, 256


def setup_inputs():
    return {"table": bf(np.random.standard_normal((S, K))), "w": bf(np.random.standard_normal((K, M)) / np.sqrt(D * K)), "b": f32(0.5 * np.random.standard_normal((M, 1))), "offs": striped(np.random.permutation(np.tile(np.arange(S), 2))[:N])}


def reference(table, w, b, offs):
    idx = offs[:16].T.reshape(-1)
    x = f64(table)[idx].T
    y = f64(w).T @ sum(x[:, t * V : (t + 1) * V] for t in range(D))
    return np.tanh(y + f64(b))

@@ -1,0 +1,75 @@
+import concourse.mybir as mybir
+from concourse.masks import make_identity
+
+P = 128
+S, K, M = 2048, 256, 128
+V, D = 256, 4
+K_BLOCKS = K // P
+ROW_BLOCKS = S // P
+CHUNK = 4
+CHUNKS = ROW_BLOCKS // CHUNK
+COLS_PER_PIECE = V // 16
+
+FLOPS = 2 * K * M * V * D
+
+BF16, F32, U16 = mybir.dt.bfloat16, mybir.dt.float32, mybir.dt.uint16
+
+
+def tile_gather_matmul_kernel(tc, table, w, b, offs, out):
+    nc = tc.nc
+    with (
+        tc.tile_pool(name="held", bufs=1) as held,
+        tc.psum_pool(name="flips", bufs=3) as flips,
+        tc.psum_pool(name="sums", bufs=1) as sums,
+    ):
+        offsets = held.tile([P, D * COLS_PER_PIECE], U16, name="offsets")
+        nc.sync.dma_start(offsets[:], offs)
+
+        rows = []
+        for c in range(CHUNKS):
+            chunk_rows = held.tile([P, CHUNK, K], BF16, name="rows%d" % c)
+            nc.sync.dma_start(
+                chunk_rows[:],
+                table[c * CHUNK * P : (c + 1) * CHUNK * P, :].rearrange("(n p) k -> p n k", p=P),
+            )
+            rows.append(chunk_rows)
+
+        weights = held.tile([P, K_BLOCKS, M], BF16, name="weights")
+        nc.scalar.dma_start(weights[:], w.rearrange("(a p) m -> p a m", p=P))
+        bias = held.tile([P, 1], F32, name="bias")
+        nc.scalar.dma_start(bias[:], b)
+
+        identity = held.tile([P, P], BF16, name="identity")
+        make_identity(nc, identity[:])
+
+        features = [held.tile([P, S], BF16, name="features%d" % a) for a in range(K_BLOCKS)]
+        for c in range(CHUNKS):
+            for a in range(K_BLOCKS):
+                flipped = flips.tile([P, CHUNK * P], BF16, name="flipped%d" % a)
+                for n in range(CHUNK):
+                    nc.tensor.transpose(
+                        flipped[:, n * P : (n + 1) * P],
+                        rows[c][:, n, a * P : (a + 1) * P],
+                        identity[:],
+                    )
+                target = features[a][:, c * CHUNK * P : (c + 1) * CHUNK * P]
+                if a == 0:
+                    nc.vector.tensor_copy(target, flipped[:])
+                else:
+                    nc.scalar.copy(target, flipped[:])
+
+        total = sums.tile([P, V], F32, name="total")
+        steps = [(a, t) for a in range(K_BLOCKS) for t in range(D)]
+        for i, (a, t) in enumerate(steps):
+            piece = offsets[:, t * COLS_PER_PIECE : (t + 1) * COLS_PER_PIECE]
+            nc.tensor.matmul(
+                total[:],
+                weights[:, a, :],
+                features[a][:].indirect(piece),
+                start=(i == 0),
+                stop=(i == len(steps) - 1),
+            )
+
+        result = held.tile([P, V], F32, name="result")
+        nc.scalar.activation(result[:], total[:], mybir.ActivationFunctionType.Tanh, bias=bias[:, 0:1])
+        nc.sync.dma_start(out, result[:])

@@ -9,6 +9,8 @@ ROW_BLOCKS = S // P
 CHUNK = 4
 CHUNKS = ROW_BLOCKS // CHUNK
 COLS_PER_PIECE = V // 16
+BANK = 512
+HEAD_WARMERS = 5
 
 FLOPS = 2 * K * M * V * D
 
@@ -42,6 +44,16 @@ def tile_gather_matmul_kernel(tc, table, w, b, offs, out):
         identity = held.tile([P, P], BF16, name="identity")
         make_identity(nc, identity[:])
 
+        zeros = held.tile([P, BANK], BF16, name="zeros")
+        nc.vector.memset(zeros[:], 0.0)
+        unread = sums.tile([P, BANK], F32, name="unread")
+
+        def keep_tensor_engine_busy():
+            nc.tensor.matmul(unread[:], zeros[:, 0:P], zeros[:], start=True, stop=True)
+
+        for i in range(HEAD_WARMERS):
+            keep_tensor_engine_busy()
+
         features = [held.tile([P, S], BF16, name="features%d" % a) for a in range(K_BLOCKS)]
         for c in range(CHUNKS):
             for a in range(K_BLOCKS):
@@ -57,6 +69,8 @@ def tile_gather_matmul_kernel(tc, table, w, b, offs, out):
                     nc.vector.tensor_copy(target, flipped[:])
                 else:
                     nc.scalar.copy(target, flipped[:])
+            if c < CHUNKS - 1:
+                keep_tensor_engine_busy()
 
         total = sums.tile([P, V], F32, name="total")
         steps = [(a, t) for a in range(K_BLOCKS) for t in range(D)]

@@ -9,8 +9,6 @@ ROW_BLOCKS = S // P
 CHUNK = 4
 CHUNKS = ROW_BLOCKS // CHUNK
 COLS_PER_PIECE = V // 16
-BANK = 512
-HEAD_WARMERS = 5
 
 FLOPS = 2 * K * M * V * D
 
@@ -21,7 +19,7 @@ def tile_gather_matmul_kernel(tc, table, w, b, offs, out):
     nc = tc.nc
     with (
         tc.tile_pool(name="held", bufs=1) as held,
-        tc.psum_pool(name="flips", bufs=3) as flips,
+        tc.psum_pool(name="flips", bufs=6) as flips,
         tc.psum_pool(name="sums", bufs=1) as sums,
     ):
         offsets = held.tile([P, D * COLS_PER_PIECE], U16, name="offsets")
@@ -32,7 +30,7 @@ def tile_gather_matmul_kernel(tc, table, w, b, offs, out):
             chunk_rows = held.tile([P, CHUNK, K], BF16, name="rows%d" % c)
             nc.sync.dma_start(
                 chunk_rows[:],
-                table[c * CHUNK * P : (c + 1) * CHUNK * P, :].rearrange("(n p) k -> p n k", p=P),
+                table[c * CHUNK * P : (c + 1) * CHUNK * P, :].rearrange("(p n) k -> p n k", p=P),
             )
             rows.append(chunk_rows)
 
@@ -44,33 +42,24 @@ def tile_gather_matmul_kernel(tc, table, w, b, offs, out):
         identity = held.tile([P, P], BF16, name="identity")
         make_identity(nc, identity[:])
 
-        zeros = held.tile([P, BANK], BF16, name="zeros")
-        nc.vector.memset(zeros[:], 0.0)
-        unread = sums.tile([P, BANK], F32, name="unread")
-
-        def keep_tensor_engine_busy():
-            nc.tensor.matmul(unread[:], zeros[:, 0:P], zeros[:], start=True, stop=True)
-
-        for i in range(HEAD_WARMERS):
-            keep_tensor_engine_busy()
-
         features = [held.tile([P, S], BF16, name="features%d" % a) for a in range(K_BLOCKS)]
         for c in range(CHUNKS):
             for a in range(K_BLOCKS):
-                flipped = flips.tile([P, CHUNK * P], BF16, name="flipped%d" % a)
+                flipped = flips.tile([P, CHUNK * P], BF16, name="flipped")
                 for n in range(CHUNK):
                     nc.tensor.transpose(
                         flipped[:, n * P : (n + 1) * P],
                         rows[c][:, n, a * P : (a + 1) * P],
                         identity[:],
                     )
-                target = features[a][:, c * CHUNK * P : (c + 1) * CHUNK * P]
-                if a == 0:
-                    nc.vector.tensor_copy(target, flipped[:])
+                in_order = flipped[:].rearrange("f (n p) -> f p n", n=CHUNK)
+                target = features[a][:, c * CHUNK * P : (c + 1) * CHUNK * P].rearrange(
+                    "f (p n) -> f p n", n=CHUNK
+                )
+                if (c * K_BLOCKS + a) % 3 == 2:
+                    nc.scalar.copy(target, in_order)
                 else:
-                    nc.scalar.copy(target, flipped[:])
-            if c < CHUNKS - 1:
-                keep_tensor_engine_busy()
+                    nc.vector.tensor_copy(target, in_order)
 
         total = sums.tile([P, V], F32, name="total")
         steps = [(a, t) for a in range(K_BLOCKS) for t in range(D)]

@@ -4,9 +4,9 @@ from concourse.masks import make_identity
 P = 128
 S, K, M = 2048, 256, 128
 V, D = 256, 4
-K_BLOCKS = K // P
+PAIR = 2
 ROW_BLOCKS = S // P
-CHUNK = 4
+CHUNK = 2
 CHUNKS = ROW_BLOCKS // CHUNK
 COLS_PER_PIECE = V // 16
 
@@ -22,53 +22,46 @@ def tile_gather_matmul_kernel(tc, table, w, b, offs, out):
         tc.psum_pool(name="flips", bufs=6) as flips,
         tc.psum_pool(name="sums", bufs=1) as sums,
     ):
-        offsets = held.tile([P, D * COLS_PER_PIECE], U16, name="offsets")
-        nc.sync.dma_start(offsets[:], offs)
-
         rows = []
         for c in range(CHUNKS):
             chunk_rows = held.tile([P, CHUNK, K], BF16, name="rows%d" % c)
             nc.sync.dma_start(
                 chunk_rows[:],
-                table[c * CHUNK * P : (c + 1) * CHUNK * P, :].rearrange("(p n) k -> p n k", p=P),
+                table[c * CHUNK * P : (c + 1) * CHUNK * P, :].rearrange("(n p) k -> p n k", p=P),
             )
             rows.append(chunk_rows)
 
-        weights = held.tile([P, K_BLOCKS, M], BF16, name="weights")
-        nc.scalar.dma_start(weights[:], w.rearrange("(a p) m -> p a m", p=P))
-        bias = held.tile([P, 1], F32, name="bias")
-        nc.scalar.dma_start(bias[:], b)
+        weights = held.tile([P, PAIR, M], BF16, name="weights")
+        nc.sync.dma_start(weights[:], w.rearrange("(j e) m -> j e m", e=PAIR))
 
-        identity = held.tile([P, P], BF16, name="identity")
+        offsets = held.tile([P, D * COLS_PER_PIECE], U16, name="offsets")
+        nc.sync.dma_start(offsets[:], offs)
+        bias = held.tile([P, 1], F32, name="bias")
+        nc.sync.dma_start(bias[:], b)
+
+        identity = held.tile([P, P], F32, name="identity")
         make_identity(nc, identity[:])
 
-        features = [held.tile([P, S], BF16, name="features%d" % a) for a in range(K_BLOCKS)]
+        features = [held.tile([P, S], BF16, name="features%d" % e) for e in range(PAIR)]
         for c in range(CHUNKS):
-            for a in range(K_BLOCKS):
-                flipped = flips.tile([P, CHUNK * P], BF16, name="flipped")
-                for n in range(CHUNK):
-                    nc.tensor.transpose(
-                        flipped[:, n * P : (n + 1) * P],
-                        rows[c][:, n, a * P : (a + 1) * P],
-                        identity[:],
-                    )
-                in_order = flipped[:].rearrange("f (n p) -> f p n", n=CHUNK)
-                target = features[a][:, c * CHUNK * P : (c + 1) * CHUNK * P].rearrange(
-                    "f (p n) -> f p n", n=CHUNK
+            words = flips.tile([P, CHUNK * P], F32, name="words")
+            for n in range(CHUNK):
+                nc.tensor.transpose(
+                    words[:, n * P : (n + 1) * P], rows[c][:, n, :].bitcast(F32), identity[:]
                 )
-                if (c * K_BLOCKS + a) % 3 == 2:
-                    nc.scalar.copy(target, in_order)
-                else:
-                    nc.vector.tensor_copy(target, in_order)
+            halves = words[:].bitcast(BF16).rearrange("j (s e) -> j e s", e=PAIR)
+            chunk_cols = slice(c * CHUNK * P, (c + 1) * CHUNK * P)
+            nc.vector.tensor_copy(features[0][:, chunk_cols], halves[:, 0, :])
+            nc.scalar.copy(features[1][:, chunk_cols], halves[:, 1, :])
 
         total = sums.tile([P, V], F32, name="total")
-        steps = [(a, t) for a in range(K_BLOCKS) for t in range(D)]
-        for i, (a, t) in enumerate(steps):
+        steps = [(e, t) for e in range(PAIR) for t in range(D)]
+        for i, (e, t) in enumerate(steps):
             piece = offsets[:, t * COLS_PER_PIECE : (t + 1) * COLS_PER_PIECE]
             nc.tensor.matmul(
                 total[:],
-                weights[:, a, :],
-                features[a][:].indirect(piece),
+                weights[:, e, :],
+                features[e][:].indirect(piece),
                 start=(i == 0),
                 stop=(i == len(steps) - 1),
             )

@@ -27,7 +27,7 @@ def tile_gather_matmul_kernel(tc, table, w, b, offs, out):
             chunk_rows = held.tile([P, CHUNK, K], BF16, name="rows%d" % c)
             nc.sync.dma_start(
                 chunk_rows[:],
-                table[c * CHUNK * P : (c + 1) * CHUNK * P, :].rearrange("(n p) k -> p n k", p=P),
+                table[c * CHUNK * P : (c + 1) * CHUNK * P, :].rearrange("(p n) k -> p n k", p=P),
             )
             rows.append(chunk_rows)
 
@@ -49,10 +49,11 @@ def tile_gather_matmul_kernel(tc, table, w, b, offs, out):
                 nc.tensor.transpose(
                     words[:, n * P : (n + 1) * P], rows[c][:, n, :].bitcast(F32), identity[:]
                 )
-            halves = words[:].bitcast(BF16).rearrange("j (s e) -> j e s", e=PAIR)
+            halves = words[:].bitcast(BF16).rearrange("j (n p e) -> j e p n", n=CHUNK, e=PAIR)
             chunk_cols = slice(c * CHUNK * P, (c + 1) * CHUNK * P)
-            nc.vector.tensor_copy(features[0][:, chunk_cols], halves[:, 0, :])
-            nc.scalar.copy(features[1][:, chunk_cols], halves[:, 1, :])
+            in_order = [features[e][:, chunk_cols].rearrange("j (p n) -> j p n", n=CHUNK) for e in range(PAIR)]
+            nc.vector.tensor_copy(in_order[0], halves[:, 0, :, :])
+            nc.scalar.copy(in_order[1], halves[:, 1, :, :])
 
         total = sums.tile([P, V], F32, name="total")
         steps = [(e, t) for e in range(PAIR) for t in range(D)]

@@ -5,10 +5,11 @@ P = 128
 S, K, M = 2048, 256, 128
 V, D = 256, 4
 PAIR = 2
-ROW_BLOCKS = S // P
-CHUNK = 2
-CHUNKS = ROW_BLOCKS // CHUNK
 COLS_PER_PIECE = V // 16
+CHUNK_ROWS = (2, 2, 2, 2, 2, 2, 2, 2)
+assert sum(CHUNK_ROWS) * P == S
+BANK = 512
+HEAD_WARMERS = 3
 
 FLOPS = 2 * K * M * V * D
 
@@ -21,15 +22,25 @@ def tile_gather_matmul_kernel(tc, table, w, b, offs, out):
         tc.tile_pool(name="held", bufs=1) as held,
         tc.psum_pool(name="flips", bufs=6) as flips,
         tc.psum_pool(name="sums", bufs=1) as sums,
+        tc.psum_pool(name="idle", bufs=1) as idle,
     ):
+        unread = idle.tile([P, BANK], F32, name="unread")
+        zeros = held.tile([P, BANK], BF16, name="zeros")
+        nc.vector.memset(zeros[:], 0.0)
+        for i in range(HEAD_WARMERS):
+            nc.tensor.matmul(unread[:], zeros[:, 0:P], zeros[:], start=True, stop=True)
+
         rows = []
-        for c in range(CHUNKS):
-            chunk_rows = held.tile([P, CHUNK, K], BF16, name="rows%d" % c)
+        starts = []
+        first = 0
+        for c, n in enumerate(CHUNK_ROWS):
+            chunk_rows = held.tile([P, n, K], BF16, name="rows%d" % c)
             nc.sync.dma_start(
-                chunk_rows[:],
-                table[c * CHUNK * P : (c + 1) * CHUNK * P, :].rearrange("(p n) k -> p n k", p=P),
+                chunk_rows[:], table[first : first + n * P, :].rearrange("(p i) k -> p i k", p=P)
             )
             rows.append(chunk_rows)
+            starts.append(first)
+            first += n * P
 
         weights = held.tile([P, PAIR, M], BF16, name="weights")
         nc.sync.dma_start(weights[:], w.rearrange("(j e) m -> j e m", e=PAIR))
@@ -43,28 +54,28 @@ def tile_gather_matmul_kernel(tc, table, w, b, offs, out):
         make_identity(nc, identity[:])
 
         features = [held.tile([P, S], BF16, name="features%d" % e) for e in range(PAIR)]
-        for c in range(CHUNKS):
-            words = flips.tile([P, CHUNK * P], F32, name="words")
-            for n in range(CHUNK):
+        for c, n in enumerate(CHUNK_ROWS):
+            words = flips.tile([P, n * P], F32, name="words")
+            for i in range(n):
                 nc.tensor.transpose(
-                    words[:, n * P : (n + 1) * P], rows[c][:, n, :].bitcast(F32), identity[:]
+                    words[:, i * P : (i + 1) * P], rows[c][:, i, :].bitcast(F32), identity[:]
                 )
-            halves = words[:].bitcast(BF16).rearrange("j (n p e) -> j e p n", n=CHUNK, e=PAIR)
-            chunk_cols = slice(c * CHUNK * P, (c + 1) * CHUNK * P)
-            in_order = [features[e][:, chunk_cols].rearrange("j (p n) -> j p n", n=CHUNK) for e in range(PAIR)]
+            halves = words[:].bitcast(BF16).rearrange("j (i p e) -> j e p i", i=n, e=PAIR)
+            chunk_cols = slice(starts[c], starts[c] + n * P)
+            in_order = [features[e][:, chunk_cols].rearrange("j (p i) -> j p i", i=n) for e in range(PAIR)]
             nc.vector.tensor_copy(in_order[0], halves[:, 0, :, :])
             nc.scalar.copy(in_order[1], halves[:, 1, :, :])
 
         total = sums.tile([P, V], F32, name="total")
         steps = [(e, t) for e in range(PAIR) for t in range(D)]
-        for i, (e, t) in enumerate(steps):
+        for step, (e, t) in enumerate(steps):
             piece = offsets[:, t * COLS_PER_PIECE : (t + 1) * COLS_PER_PIECE]
             nc.tensor.matmul(
                 total[:],
                 weights[:, e, :],
                 features[e][:].indirect(piece),
-                start=(i == 0),
-                stop=(i == len(steps) - 1),
+                start=(step == 0),
+                stop=(step == len(steps) - 1),
             )
 
         result = held.tile([P, V], F32, name="result")

import concourse.mybir as mybir
from concourse.masks import make_identity

P = 128
S, K, M = 2048, 256, 128
V, D = 256, 4
PAIR = 2
COLS_PER_PIECE = V // 16
CHUNK_ROWS = (2, 2, 2, 2, 2, 2, 2, 2)
assert sum(CHUNK_ROWS) * P == S
BANK = 512
HEAD_WARMERS = 3

FLOPS = 2 * K * M * V * D

BF16, F32, U16 = mybir.dt.bfloat16, mybir.dt.float32, mybir.dt.uint16


def tile_gather_matmul_kernel(tc, table, w, b, offs, out):
    nc = tc.nc
    with (
        tc.tile_pool(name="held", bufs=1) as held,
        tc.psum_pool(name="flips", bufs=6) as flips,
        tc.psum_pool(name="sums", bufs=1) as sums,
        tc.psum_pool(name="idle", bufs=1) as idle,
    ):
        unread = idle.tile([P, BANK], F32, name="unread")
        zeros = held.tile([P, BANK], BF16, name="zeros")
        nc.vector.memset(zeros[:], 0.0)
        for i in range(HEAD_WARMERS):
            nc.tensor.matmul(unread[:], zeros[:, 0:P], zeros[:], start=True, stop=True)

        rows = []
        starts = []
        first = 0
        for c, n in enumerate(CHUNK_ROWS):
            chunk_rows = held.tile([P, n, K], BF16, name="rows%d" % c)
            nc.sync.dma_start(
                chunk_rows[:], table[first : first + n * P, :].rearrange("(p i) k -> p i k", p=P)
            )
            rows.append(chunk_rows)
            starts.append(first)
            first += n * P

        weights = held.tile([P, PAIR, M], BF16, name="weights")
        nc.sync.dma_start(weights[:], w.rearrange("(j e) m -> j e m", e=PAIR))

        offsets = held.tile([P, D * COLS_PER_PIECE], U16, name="offsets")
        nc.sync.dma_start(offsets[:], offs)
        bias = held.tile([P, 1], F32, name="bias")
        nc.sync.dma_start(bias[:], b)

        identity = held.tile([P, P], F32, name="identity")
        make_identity(nc, identity[:])

        features = [held.tile([P, S], BF16, name="features%d" % e) for e in range(PAIR)]
        for c, n in enumerate(CHUNK_ROWS):
            words = flips.tile([P, n * P], F32, name="words")
            for i in range(n):
                nc.tensor.transpose(
                    words[:, i * P : (i + 1) * P], rows[c][:, i, :].bitcast(F32), identity[:]
                )
            halves = words[:].bitcast(BF16).rearrange("j (i p e) -> j e p i", i=n, e=PAIR)
            chunk_cols = slice(starts[c], starts[c] + n * P)
            in_order = [features[e][:, chunk_cols].rearrange("j (p i) -> j p i", i=n) for e in range(PAIR)]
            nc.vector.tensor_copy(in_order[0], halves[:, 0, :, :])
            nc.scalar.copy(in_order[1], halves[:, 1, :, :])

        total = sums.tile([P, V], F32, name="total")
        steps = [(e, t) for e in range(PAIR) for t in range(D)]
        for step, (e, t) in enumerate(steps):
            piece = offsets[:, t * COLS_PER_PIECE : (t + 1) * COLS_PER_PIECE]
            nc.tensor.matmul(
                total[:],
                weights[:, e, :],
                features[e][:].indirect(piece),
                start=(step == 0),
                stop=(step == len(steps) - 1),
            )

        result = held.tile([P, V], F32, name="result")
        nc.scalar.activation(result[:], total[:], mybir.ActivationFunctionType.Tanh, bias=bias[:, 0:1])
        nc.sync.dma_start(out, result[:])
